import numpy as np
import ml_dtypes


def mxq(x, axis, fmt="e4m3"):
    dtype, down = {"e4m3": (ml_dtypes.float8_e4m3fn, 7), "e5m2": (ml_dtypes.float8_e5m2, 14)}[fmt]
    v = np.moveaxis(np.asarray(x, np.float32).astype(ml_dtypes.bfloat16).astype(np.float64), axis, -1)
    blocks = v.reshape(v.shape[:-1] + (-1, 32))
    amax = np.abs(blocks).max(-1, keepdims=True)
    byte = np.maximum(np.where(amax > 0, np.frexp(amax)[1] - 1 + 127, 0) - down, 1)
    scale = np.exp2(byte - 127.0)
    codes = (blocks / scale).astype(np.float32).astype(dtype).astype(np.float64)
    return np.moveaxis((codes * scale).reshape(v.shape), -1, axis)


WIDE = False


def mx_kscale(k):
    if not WIDE:
        return np.ones(k)
    levels = np.array([30, -30])
    if k % 512:
        return np.exp2(np.random.permutation(np.resize(levels, k // 32))).repeat(32)
    a = np.empty((k // 512, 16))
    for p in range(k // 512):
        a[p, :8] = np.random.permutation(np.resize(levels, 8))
        for g in range(8):
            far = levels[np.abs(levels - a[p, g]) >= 10]
            a[p, g + 8] = far[np.random.randint(len(far))]
    return np.exp2(a.ravel()).repeat(32)


def f64(x):
    return np.asarray(x).astype(np.float64)


def striped(idx):
    return np.tile(idx.reshape(-1, 16).T, (8, 1)).astype(np.uint16)


def unstriped(offs):
    return offs[:16].T.reshape(-1).astype(np.int64)


E2M1 = np.array([0.0, 0.5, 1.0, 1.5, 2.0, 3.0, 4.0, 6.0, -0.0, -0.5, -1.0, -1.5, -2.0, -3.0, -4.0, -6.0])


def pack_weight(w, fmt):
    k, n = w.shape
    w = f64(np.asarray(w, np.float32).astype(ml_dtypes.bfloat16)).reshape(k // 32, 32, n)
    amax = np.abs(w).max(1)
    if fmt == "e4m3":
        byte = np.frexp(amax)[1] - 1 + 127 - 7
    else:
        mant, ex = np.frexp(amax / 6.0)
        byte = np.where(mant > 0.5, ex, ex - 1) + 127
    byte = np.clip(np.where(amax > 0, byte, 1), 1, 254)
    scaled = (w * np.exp2(127.0 - byte)[:, None, :]).reshape(k, n).astype(np.float32)
    by_word = np.ascontiguousarray(scaled.reshape(k // 512, 128, 4, n).transpose(0, 1, 3, 2))
    if fmt == "e4m3":
        words = by_word.astype(ml_dtypes.float8_e4m3fn).view(np.uint8)
    else:
        c = by_word.astype(ml_dtypes.float4_e2m1fn).view(np.uint8) & 0xF
        words = (c[..., 0::2] | (c[..., 1::2] << 4)).reshape(k // 512, 128, 2 * n)
    return np.ascontiguousarray(words), np.ascontiguousarray(byte.astype(np.uint8).reshape(k // 512, 16, n))


def unpack_weight(words, scales, fmt):
    g, _, n = scales.shape
    words = np.ascontiguousarray(words).reshape(g, 128, n, -1)
    if fmt == "e4m3":
        vals = words.view(ml_dtypes.float8_e4m3fn).astype(np.float64)
    else:
        nib = np.empty((g, 128, n, 4), np.uint8)
        nib[..., 0::2] = words & 0xF
        nib[..., 1::2] = words >> 4
        vals = E2M1[nib]
    vals = vals * np.repeat(np.exp2(scales.astype(np.float64) - 127.0), 8, axis=1)[..., None]
    return vals.transpose(0, 1, 3, 2).reshape(g * 512, n)


def planes(y):
    n, m = y.shape
    v = y.astype(np.float32).astype(ml_dtypes.bfloat16).astype(np.float64).reshape(n // 32, 32, m)
    top = np.abs(v).max(1)
    byte = np.clip(np.where(top > 0, np.frexp(top)[1] - 1 + 127 - 7, 1), 1, 254)
    codes = (v * np.exp2(127.0 - byte)[:, None, :]).reshape(n, m).astype(np.float32).astype(ml_dtypes.float8_e4m3fn).view(np.uint8)
    words = codes.reshape(n // 512, 128, 4, m).transpose(0, 1, 3, 2)
    return np.ascontiguousarray(words), np.ascontiguousarray(byte.astype(np.uint8).reshape(n // 512, 16, m))


K, N, T, J = 512, 512, 2048, 1024


def setup_inputs():
    n = np.random.standard_normal
    s = mx_kscale(K)[:, None]
    m = np.exp(0.5 * n((1, J)))
    w = n((K, N)) / np.sqrt(K) / s
    w4 = pack_weight(w, "e2m1")
    wrest = w - unpack_weight(*w4, "e2m1")
    p_w8 = pack_weight(wrest, "e4m3")
    return {
        "dy": (m * n((K, J)) * s).astype(np.float32),
        "w4_words": w4[0],
        "w4_scales": w4[1],
        "w8_words": p_w8[0],
        "w8_scales": p_w8[1],
        "d": (0.5 + 0.3 * n((N, J))).astype(np.float32),
        "wgo": np.tile(np.random.uniform(0.5, 2.0, J), (128, 1)).astype(np.float32),
        "offs": striped(np.random.permutation(T)[:J]),
    }


def reference(dy, w4_words, w4_scales, w8_words, w8_scales, d, wgo, offs):
    idx = unstriped(offs)
    dy_ = mxq(f64(dy), 0, "e5m2")
    w4_ = unpack_weight(w4_words, w4_scales, "e2m1")
    w8_ = unpack_weight(w8_words, w8_scales, "e4m3")
    dx = w4_.T @ dy_ + w8_.T @ dy_
    out = np.zeros((N, T))
    out[:, idx] = f64(wgo)[0] * (dx * f64(d))
    return (out,) + planes(out)

@@ -1,0 +1,188 @@
+from contextlib import ExitStack
+
+import concourse.mybir as mybir
+from concourse.masks import make_identity
+
+K, N, T, J = 512, 512, 2048, 1024
+FLOPS = 2 * 2 * K * N * J
+
+F32 = mybir.dt.float32
+BF16 = mybir.dt.bfloat16
+I32 = mybir.dt.int32
+U32 = mybir.dt.uint32
+U16 = mybir.dt.uint16
+U8 = mybir.dt.uint8
+E5M2X4 = mybir.dt.float8_e5m2_x4
+E4M3X4 = mybir.dt.float8_e4m3fn_x4
+E2M1X4 = mybir.dt.float4_e2m1fn_x4
+COPY = mybir.ActivationFunctionType.Copy
+MULT = mybir.AluOpType.mult
+
+P = 128
+PACK = 4
+DY_CHUNK = 256
+PLANE_ORDER = (2, 0, 1, 3)
+FIRST_SLICES = ((0, 256), (256, 512), (512, 768), (768, 1024))
+OUT_CHUNKS = ((0, 512), (512, 896), (896, 1408), (1408, 1792), (1792, 2048))
+VECTOR_CHUNKS = 2
+
+
+def tile_list_embg_res_mulP_kernel(
+    tc, dy, w4_words, w4_scales, w8_words, w8_scales, d, wgo, offs, out_0, out_1, out_2
+):
+    nc = tc.nc
+    with ExitStack() as ctx:
+        keep = ctx.enter_context(tc.tile_pool(name="keep", bufs=1))
+        psum = ctx.enter_context(tc.psum_pool(name="psum", bufs=1))
+
+        offsets = keep.tile([P, J // 16], U16, name="offsets")
+        w_scales = keep.tile([P, 2 * N], U8, name="w_scales", align_bytes=64)
+        wgo_rows = keep.tile([P, P], F32, name="wgo_rows")
+        w4 = keep.tile([P, 2 * N], U8, name="w4", align_bytes=64)
+        w8 = keep.tile([P, N], U32, name="w8", align_bytes=64)
+        identity = keep.tile([P, P], F32, name="identity")
+        page_a = keep.tile([P, T], F32, name="page_a")
+        page_b = keep.tile([P, T], F32, name="page_b")
+
+        nc.gpsimd.memset(w_scales[:].bitcast(I32), 0)
+        nc.gpsimd.memset(wgo_rows[:], 0.0)
+        nc.gpsimd.dma_start(out=wgo_rows[0 : J // P, :], in_=wgo[0].rearrange("(c m) -> c m", m=P))
+        nc.vector.memset(page_a[:], 0.0)
+        nc.vector.memset(page_b[:], 0.0)
+        make_identity(nc, identity[:])
+
+        dy_rows = dy.rearrange("(p i) j -> p i j", i=PACK)
+        d_rows = d.rearrange("(p i) j -> p i j", i=PACK)
+        out_rows = out_0.rearrange("(p i) t -> p i t", i=PACK)
+        first = PLANE_ORDER[0]
+
+        n_chunks = J // DY_CHUNK
+        dy_raw = [keep.tile([P, PACK, DY_CHUNK], F32, name="dy_raw%d" % b) for b in range(n_chunks)]
+
+        def load_dy(b):
+            nc.sync.dma_start(out=dy_raw[b][:], in_=dy_rows[:, :, b * DY_CHUNK : (b + 1) * DY_CHUNK])
+
+        def load_scales(half, src):
+            for q in range(4):
+                nc.sync.dma_start(
+                    out=w_scales[32 * q : 32 * q + 4, half * N : (half + 1) * N].bitcast(I32),
+                    in_=src[0, 4 * q : 4 * q + 4, :].bitcast(I32),
+                )
+
+        load_scales(0, w4_scales)
+        load_dy(0)
+        nc.sync.dma_start(out=w4[:].bitcast(I32), in_=w4_words[0].bitcast(I32))
+        nc.sync.dma_start(out=w8[:].bitcast(I32), in_=w8_words[0].rearrange("p n i -> p (n i)").bitcast(I32))
+        nc.sync.dma_start(offsets[:], offs)
+        load_scales(1, w8_scales)
+        load_dy(1)
+        load_dy(2)
+        d_head = keep.tile([P, DY_CHUNK], F32, name="d_head")
+        nc.sync.dma_start(out=d_head[:], in_=d_rows[:, first, 0:DY_CHUNK])
+        load_dy(3)
+        d_rest = keep.tile([P, J - DY_CHUNK], F32, name="d_rest", tag="late_page")
+        nc.sync.dma_start(out=d_rest[:], in_=d_rows[:, first, DY_CHUNK:J])
+        d_plane = {}
+        for i in PLANE_ORDER[1:]:
+            d_plane[i] = keep.tile([P, J], F32, name="d_plane%d" % i)
+            nc.sync.dma_start(out=d_plane[i][:], in_=d_rows[:, i, :])
+
+        wgo_bank = psum.tile([P, P], F32, name="wgo_bank")
+        nc.tensor.transpose(wgo_bank[:], wgo_rows[:], identity[:])
+        wgo_col = keep.tile([P, J // P], F32, name="wgo_col")
+        nc.scalar.activation(out=wgo_col[:], in_=wgo_bank[:, 0 : J // P], func=COPY)
+
+        dy_codes, dy_scales = [], []
+        for b in range(n_chunks):
+            grouped = keep.tile([P, DY_CHUNK * PACK], BF16, name="dy_grouped%d" % b, align_bytes=64)
+            nc.vector.tensor_copy(
+                out=grouped[:].rearrange("p (c e i) -> p c i e", e=2, i=PACK),
+                in_=dy_raw[b][:].rearrange("p i (c e) -> p c i e", e=2),
+            )
+            codes = keep.tile([P, DY_CHUNK], U32, name="dy_codes%d" % b, align_bytes=64)
+            scales = keep.tile([P, DY_CHUNK], U8, name="dy_scales%d" % b, align_bytes=64)
+            nc.vector.quantize_mx(out=codes[:].bitcast(E5M2X4), scales=scales[:], in_=grouped[:])
+            dy_codes.append(codes)
+            dy_scales.append(scales)
+
+        dxw_t = []
+
+        def multiply(c):
+            b, lo = divmod(c * P, DY_CHUNK)
+            acc = psum.tile([P, N], F32, name="acc", bufs=3)
+            lhs = dy_codes[b][:, lo : lo + P].bitcast(E5M2X4)
+            lhs_scale = dy_scales[b][:, lo : lo + P]
+            nc.tensor.matmul_mx(
+                out=acc[:], lhsT=lhs, lhsT_scale=lhs_scale,
+                rhs=w4[:].bitcast(E2M1X4), rhs_scale=w_scales[:, 0:N], start=True, stop=False,
+            )
+            nc.tensor.matmul_mx(
+                out=acc[:], lhsT=lhs, lhsT_scale=lhs_scale,
+                rhs=w8[:].bitcast(E4M3X4), rhs_scale=w_scales[:, N : 2 * N], start=False, stop=True,
+            )
+            staged = keep.tile([P, PACK, P], F32, name="dxw_t%d" % c)
+            nc.scalar.activation(
+                out=staged[:], in_=acc[:].rearrange("j (p i) -> j i p", i=PACK),
+                func=COPY, scale=wgo_col[:, c : c + 1],
+            )
+            dxw_t.append(staged)
+
+        def turn(i, lo, hi, dst):
+            bank = psum.tile([P, hi - lo], F32, name="turned", bufs=4)
+            for c in range(lo // P, hi // P):
+                nc.tensor.transpose(bank[:, c * P - lo : (c + 1) * P - lo], dxw_t[c][:, i, :], identity[:])
+            nc.scalar.copy(out=dst, in_=bank[:])
+
+        first_parts = []
+        for lo, hi in FIRST_SLICES:
+            for c in range(lo // P, hi // P):
+                multiply(c)
+            part = keep.tile([P, hi - lo], F32, name="dxw_first%d" % lo)
+            turn(first, lo, hi, part[:])
+            first_parts.append(part)
+        dxw = {}
+        for i in PLANE_ORDER[1:]:
+            dxw[i] = keep.tile([P, J], F32, name="dxw%d" % i)
+            for lo in range(0, J, 512):
+                turn(i, lo, lo + 512, dxw[i][:, lo : lo + 512])
+
+        grouped_out = [
+            keep.tile([P, hi - lo, PACK], BF16, name="out_grouped%d" % lo, align_bytes=64) for lo, hi in OUT_CHUNKS
+        ]
+
+        def round_plane(i, page, on_vector):
+            for m, (lo, hi) in enumerate(OUT_CHUNKS):
+                if m < on_vector:
+                    nc.vector.tensor_copy(out=grouped_out[m][:, :, i], in_=page[:, lo:hi])
+                else:
+                    nc.scalar.copy(out=grouped_out[m][:, :, i], in_=page[:, lo:hi])
+
+        for (lo, hi), part in zip(FIRST_SLICES, first_parts):
+            d_part = d_head[:] if lo == 0 else d_rest[:, lo - DY_CHUNK : hi - DY_CHUNK]
+            nc.vector.tensor_tensor(page_a[:].indirect(offsets[:, lo // 16 : hi // 16]), part[:], d_part, MULT)
+        nc.sync.dma_start(out=out_rows[:, first, :], in_=page_a[:])
+        round_plane(first, page_a, 0)
+
+        page_c = keep.tile([P, T], F32, name="page_c", tag="late_page")
+        nc.gpsimd.memset(page_c[:], 0.0)
+
+        for i, page in zip(PLANE_ORDER[1:], (page_b, page_c, page_a)):
+            nc.vector.tensor_tensor(page[:].indirect(offsets[:]), dxw[i][:], d_plane[i][:], MULT)
+            nc.sync.dma_start(out=out_rows[:, i, :], in_=page[:])
+            round_plane(i, page, VECTOR_CHUNKS if i == PLANE_ORDER[-1] else 0)
+
+        out_scales = keep.tile([P, T], U8, name="out_scales", align_bytes=64)
+        words_hbm = out_1[0].rearrange("p t i -> p (t i)").bitcast(I32)
+        for m, (lo, hi) in enumerate(OUT_CHUNKS):
+            codes = keep.tile([P, hi - lo], U32, name="out_codes%d" % lo, align_bytes=64)
+            nc.vector.quantize_mx(
+                out=codes[:].bitcast(E4M3X4), scales=out_scales[:, lo:hi],
+                in_=grouped_out[m][:].rearrange("p t i -> p (t i)"),
+            )
+            nc.sync.dma_start(out=words_hbm[:, lo:hi], in_=codes[:].bitcast(I32))
+        for q in range(4):
+            queue = nc.scalar if q % 2 else nc.sync
+            queue.dma_start(
+                out=out_2[0, 4 * q : 4 * q + 4, :].bitcast(I32),
+                in_=out_scales[32 * q : 32 * q + 4, :].bitcast(I32),
+            )

@@ -21,10 +21,13 @@ MULT = mybir.AluOpType.mult
 P = 128
 PACK = 4
 DY_CHUNK = 256
-PLANE_ORDER = (2, 0, 1, 3)
-FIRST_SLICES = ((0, 256), (256, 512), (512, 768), (768, 1024))
+EARLY_PLANES = (2, 0)
+LATE_PLANES = (1, 3)
+EARLY_SLICES = ((0, 256), (256, 512), (512, 1024))
 OUT_CHUNKS = ((0, 512), (512, 896), (896, 1408), (1408, 1792), (1792, 2048))
 VECTOR_CHUNKS = 2
+ACC_BANK = (0, 1, 2, 3, 0, 1, 2, 3)
+LATE_BANK = (2, 3, 6, 7)
 
 
 def tile_list_embg_res_mulP_kernel(
@@ -37,24 +40,21 @@ def tile_list_embg_res_mulP_kernel(
 
         offsets = keep.tile([P, J // 16], U16, name="offsets")
         w_scales = keep.tile([P, 2 * N], U8, name="w_scales", align_bytes=64)
-        wgo_rows = keep.tile([P, P], F32, name="wgo_rows")
+        wgo_rows = keep.tile([P, 32], F32, name="wgo_rows", align_bytes=64)
         w4 = keep.tile([P, 2 * N], U8, name="w4", align_bytes=64)
         w8 = keep.tile([P, N], U32, name="w8", align_bytes=64)
         identity = keep.tile([P, P], F32, name="identity")
         page_a = keep.tile([P, T], F32, name="page_a")
         page_b = keep.tile([P, T], F32, name="page_b")
+        page_c = keep.tile([P, T], F32, name="page_c")
 
-        nc.gpsimd.memset(w_scales[:].bitcast(I32), 0)
-        nc.gpsimd.memset(wgo_rows[:], 0.0)
-        nc.gpsimd.dma_start(out=wgo_rows[0 : J // P, :], in_=wgo[0].rearrange("(c m) -> c m", m=P))
-        nc.vector.memset(page_a[:], 0.0)
-        nc.vector.memset(page_b[:], 0.0)
+        for page in (page_a, page_b, page_c):
+            nc.vector.memset(page[:].bitcast(I32), 0)
         make_identity(nc, identity[:])
 
         dy_rows = dy.rearrange("(p i) j -> p i j", i=PACK)
         d_rows = d.rearrange("(p i) j -> p i j", i=PACK)
         out_rows = out_0.rearrange("(p i) t -> p i t", i=PACK)
-        first = PLANE_ORDER[0]
 
         n_chunks = J // DY_CHUNK
         dy_raw = [keep.tile([P, PACK, DY_CHUNK], F32, name="dy_raw%d" % b) for b in range(n_chunks)]
@@ -65,53 +65,54 @@ def tile_list_embg_res_mulP_kernel(
         def load_scales(half, src):
             for q in range(4):
                 nc.sync.dma_start(
-                    out=w_scales[32 * q : 32 * q + 4, half * N : (half + 1) * N].bitcast(I32),
-                    in_=src[0, 4 * q : 4 * q + 4, :].bitcast(I32),
+                    out=w_scales[32 * q : 32 * (q + 1), half * N : (half + 1) * N].bitcast(I32),
+                    in_=src[0, 4 * q : 4 * q + 4, :].bitcast(I32).partition_broadcast(8),
                 )
 
+        nc.sync.dma_start(out=wgo_rows[:], in_=wgo.rearrange("r (c a x) -> a (r c) x", a=4, x=32)[:, 0:32, :])
         load_scales(0, w4_scales)
         load_dy(0)
         nc.sync.dma_start(out=w4[:].bitcast(I32), in_=w4_words[0].bitcast(I32))
         nc.sync.dma_start(out=w8[:].bitcast(I32), in_=w8_words[0].rearrange("p n i -> p (n i)").bitcast(I32))
-        nc.sync.dma_start(offsets[:], offs)
         load_scales(1, w8_scales)
         load_dy(1)
         load_dy(2)
-        d_head = keep.tile([P, DY_CHUNK], F32, name="d_head")
-        nc.sync.dma_start(out=d_head[:], in_=d_rows[:, first, 0:DY_CHUNK])
         load_dy(3)
-        d_rest = keep.tile([P, J - DY_CHUNK], F32, name="d_rest", tag="late_page")
-        nc.sync.dma_start(out=d_rest[:], in_=d_rows[:, first, DY_CHUNK:J])
-        d_plane = {}
-        for i in PLANE_ORDER[1:]:
-            d_plane[i] = keep.tile([P, J], F32, name="d_plane%d" % i)
-            nc.sync.dma_start(out=d_plane[i][:], in_=d_rows[:, i, :])
+        d_head = keep.tile([P, 2, DY_CHUNK], F32, name="d_head")
+        nc.sync.dma_start(out=d_head[:], in_=d_rows[:, 0:PACK:2, 0:DY_CHUNK])
+        nc.sync.dma_start(offsets[:], offs)
+        d_rest = keep.tile([P, 2, J - DY_CHUNK], F32, name="d_rest")
+        nc.sync.dma_start(out=d_rest[:], in_=d_rows[:, 0:PACK:2, DY_CHUNK:J])
 
-        wgo_bank = psum.tile([P, P], F32, name="wgo_bank")
-        nc.tensor.transpose(wgo_bank[:], wgo_rows[:], identity[:])
-        wgo_col = keep.tile([P, J // P], F32, name="wgo_col")
-        nc.scalar.activation(out=wgo_col[:], in_=wgo_bank[:, 0 : J // P], func=COPY)
+        wgo_col = keep.tile([P, 32], F32, name="wgo_col", align_bytes=64)
+        nc.vector.transpose(wgo_col[:], wgo_rows[:])
 
         dy_codes, dy_scales = [], []
+        blocks = DY_CHUNK // P
         for b in range(n_chunks):
-            grouped = keep.tile([P, DY_CHUNK * PACK], BF16, name="dy_grouped%d" % b, align_bytes=64)
-            nc.vector.tensor_copy(
-                out=grouped[:].rearrange("p (c e i) -> p c i e", e=2, i=PACK),
-                in_=dy_raw[b][:].rearrange("p i (c e) -> p c i e", e=2),
-            )
-            codes = keep.tile([P, DY_CHUNK], U32, name="dy_codes%d" % b, align_bytes=64)
-            scales = keep.tile([P, DY_CHUNK], U8, name="dy_scales%d" % b, align_bytes=64)
-            nc.vector.quantize_mx(out=codes[:].bitcast(E5M2X4), scales=scales[:], in_=grouped[:])
-            dy_codes.append(codes)
-            dy_scales.append(scales)
+            rounded = []
+            for h in range(blocks):
+                c = b * blocks + h
+                tile_c = keep.tile([P, P * PACK], BF16, name="dy_grouped%d" % c, align_bytes=64)
+                nc.vector.tensor_copy(
+                    out=tile_c[:].rearrange("p (c e i) -> p c i e", e=2, i=PACK),
+                    in_=dy_raw[b][:, :, h * P : (h + 1) * P].rearrange("p i (c e) -> p c i e", e=2),
+                )
+                rounded.append(tile_c)
+            for h in range(blocks):
+                c = b * blocks + h
+                codes = keep.tile([P, P], U32, name="dy_codes%d" % c, align_bytes=64)
+                scales = keep.tile([P, P], U8, name="dy_scales%d" % c, align_bytes=64)
+                nc.vector.quantize_mx(out=codes[:].bitcast(E5M2X4), scales=scales[:], in_=rounded[h][:])
+                dy_codes.append(codes)
+                dy_scales.append(scales)
 
         dxw_t = []
 
         def multiply(c):
-            b, lo = divmod(c * P, DY_CHUNK)
-            acc = psum.tile([P, N], F32, name="acc", bufs=3)
-            lhs = dy_codes[b][:, lo : lo + P].bitcast(E5M2X4)
-            lhs_scale = dy_scales[b][:, lo : lo + P]
+            acc = psum.tile([P, N], F32, name="acc", tag="bank%d" % ACC_BANK[c])
+            lhs = dy_codes[c][:].bitcast(E5M2X4)
+            lhs_scale = dy_scales[c][:]
             nc.tensor.matmul_mx(
                 out=acc[:], lhsT=lhs, lhsT_scale=lhs_scale,
                 rhs=w4[:].bitcast(E2M1X4), rhs_scale=w_scales[:, 0:N], start=True, stop=False,
@@ -120,56 +121,79 @@ def tile_list_embg_res_mulP_kernel(
                 out=acc[:], lhsT=lhs, lhsT_scale=lhs_scale,
                 rhs=w8[:].bitcast(E4M3X4), rhs_scale=w_scales[:, N : 2 * N], start=False, stop=True,
             )
-            staged = keep.tile([P, PACK, P], F32, name="dxw_t%d" % c)
+            staged = keep.tile([P, PACK, P], F32, name="dxw_t%d" % c, tag="dxw_t%d" % c, align_bytes=64)
             nc.scalar.activation(
                 out=staged[:], in_=acc[:].rearrange("j (p i) -> j i p", i=PACK),
                 func=COPY, scale=wgo_col[:, c : c + 1],
             )
             dxw_t.append(staged)
 
-        def turn(i, lo, hi, dst):
-            bank = psum.tile([P, hi - lo], F32, name="turned", bufs=4)
+        def turn(i, lo, hi, dst, bank_no):
+            bank = psum.tile([P, hi - lo], F32, name="turned", tag="bank%d" % bank_no)
             for c in range(lo // P, hi // P):
                 nc.tensor.transpose(bank[:, c * P - lo : (c + 1) * P - lo], dxw_t[c][:, i, :], identity[:])
             nc.scalar.copy(out=dst, in_=bank[:])
 
-        first_parts = []
-        for lo, hi in FIRST_SLICES:
+        early_parts = {}
+        for s, (lo, hi) in enumerate(EARLY_SLICES):
             for c in range(lo // P, hi // P):
                 multiply(c)
-            part = keep.tile([P, hi - lo], F32, name="dxw_first%d" % lo)
-            turn(first, lo, hi, part[:])
-            first_parts.append(part)
-        dxw = {}
-        for i in PLANE_ORDER[1:]:
-            dxw[i] = keep.tile([P, J], F32, name="dxw%d" % i)
-            for lo in range(0, J, 512):
-                turn(i, lo, lo + 512, dxw[i][:, lo : lo + 512])
+            for a, i in enumerate(EARLY_PLANES):
+                early_parts[i, lo] = keep.tile([P, hi - lo], F32, name="dxw%d_%d" % (i, lo))
+                turn(i, lo, hi, early_parts[i, lo][:], 2 + 2 * s + a)
+        dxw_late = {}
+        for a, i in enumerate(LATE_PLANES):
+            dxw_late[i] = keep.tile([P, J], F32, name="dxw%d" % i)
+            for h in range(2):
+                turn(i, h * N, (h + 1) * N, dxw_late[i][:, h * N : (h + 1) * N], LATE_BANK[2 * a + h])
 
-        grouped_out = [
-            keep.tile([P, hi - lo, PACK], BF16, name="out_grouped%d" % lo, align_bytes=64) for lo, hi in OUT_CHUNKS
-        ]
+        d_late = {}
+        for a, i in enumerate(LATE_PLANES):
+            d_late[i] = keep.tile([P, J], F32, name="d_late%d" % i, tag="dxw_t%d" % (J // P - 2 - a), align_bytes=64)
+            nc.scalar.dma_start(out=d_late[i][:], in_=d_rows[:, i, :])
 
-        def round_plane(i, page, on_vector):
-            for m, (lo, hi) in enumerate(OUT_CHUNKS):
-                if m < on_vector:
-                    nc.vector.tensor_copy(out=grouped_out[m][:, :, i], in_=page[:, lo:hi])
-                else:
-                    nc.scalar.copy(out=grouped_out[m][:, :, i], in_=page[:, lo:hi])
+        grouped_all = keep.tile([P, T * PACK], BF16, name="out_grouped", tag="dxw_t%d" % (J // P - 1), align_bytes=64)
 
-        for (lo, hi), part in zip(FIRST_SLICES, first_parts):
-            d_part = d_head[:] if lo == 0 else d_rest[:, lo - DY_CHUNK : hi - DY_CHUNK]
-            nc.vector.tensor_tensor(page_a[:].indirect(offsets[:, lo // 16 : hi // 16]), part[:], d_part, MULT)
-        nc.sync.dma_start(out=out_rows[:, first, :], in_=page_a[:])
-        round_plane(first, page_a, 0)
+        def grouped(lo, hi):
+            return grouped_all[:, lo * PACK : hi * PACK].rearrange("p (t i) -> p t i", i=PACK)
 
-        page_c = keep.tile([P, T], F32, name="page_c", tag="late_page")
-        nc.gpsimd.memset(page_c[:], 0.0)
+        split = OUT_CHUNKS[VECTOR_CHUNKS][0]
+        staged_chunks = range(VECTOR_CHUNKS, len(OUT_CHUNKS))
+        pair = {}
+        for m in staged_chunks:
+            pair[m] = keep.tile([P, 2, OUT_CHUNKS[m][1] - OUT_CHUNKS[m][0]], F32, name="pair%d" % m)
+        pages = dict(zip(EARLY_PLANES + LATE_PLANES, (page_a, page_b, page_c, page_a)))
 
-        for i, page in zip(PLANE_ORDER[1:], (page_b, page_c, page_a)):
-            nc.vector.tensor_tensor(page[:].indirect(offsets[:]), dxw[i][:], d_plane[i][:], MULT)
-            nc.sync.dma_start(out=out_rows[:, i, :], in_=page[:])
-            round_plane(i, page, VECTOR_CHUNKS if i == PLANE_ORDER[-1] else 0)
+        def round_columns(copy, i, lo, hi):
+            copy(out=grouped(lo, hi)[:, :, i], in_=pages[i][:, lo:hi])
+
+        for lo, hi in EARLY_SLICES:
+            for i in EARLY_PLANES:
+                d_part = d_head[:, i // 2, :] if lo == 0 else d_rest[:, i // 2, lo - DY_CHUNK : hi - DY_CHUNK]
+                nc.vector.tensor_tensor(
+                    pages[i][:].indirect(offsets[:, lo // 16 : hi // 16]), early_parts[i, lo][:], d_part, MULT
+                )
+        for i in EARLY_PLANES:
+            for m in staged_chunks:
+                lo, hi = OUT_CHUNKS[m]
+                nc.sync.dma_start(out=pair[m][:, i // 2, :], in_=pages[i][:, lo:hi])
+        for i in EARLY_PLANES:
+            nc.sync.dma_start(out=out_rows[:, i, :], in_=pages[i][:])
+            round_columns(nc.scalar.copy, i, 0, split)
+        for m in staged_chunks:
+            nc.scalar.copy(
+                out=grouped(*OUT_CHUNKS[m])[:, :, 0:PACK:2].rearrange("p (c e) a -> p c a e", e=2),
+                in_=pair[m][:].rearrange("p a (c e) -> p c a e", e=2),
+            )
+
+        for i in LATE_PLANES:
+            nc.vector.tensor_tensor(pages[i][:].indirect(offsets[:]), dxw_late[i][:], d_late[i][:], MULT)
+            nc.sync.dma_start(out=out_rows[:, i, :], in_=pages[i][:])
+            if i == LATE_PLANES[0]:
+                round_columns(nc.scalar.copy, i, 0, T)
+            else:
+                for m, (lo, hi) in enumerate(OUT_CHUNKS):
+                    round_columns(nc.vector.tensor_copy if m < VECTOR_CHUNKS else nc.scalar.copy, i, lo, hi)
 
         out_scales = keep.tile([P, T], U8, name="out_scales", align_bytes=64)
         words_hbm = out_1[0].rearrange("p t i -> p (t i)").bitcast(I32)
@@ -177,12 +201,11 @@ def tile_list_embg_res_mulP_kernel(
             codes = keep.tile([P, hi - lo], U32, name="out_codes%d" % lo, align_bytes=64)
             nc.vector.quantize_mx(
                 out=codes[:].bitcast(E4M3X4), scales=out_scales[:, lo:hi],
-                in_=grouped_out[m][:].rearrange("p t i -> p (t i)"),
+                in_=grouped_all[:, lo * PACK : hi * PACK],
             )
             nc.sync.dma_start(out=words_hbm[:, lo:hi], in_=codes[:].bitcast(I32))
         for q in range(4):
-            queue = nc.scalar if q % 2 else nc.sync
-            queue.dma_start(
+            nc.sync.dma_start(
                 out=out_2[0, 4 * q : 4 * q + 4, :].bitcast(I32),
                 in_=out_scales[32 * q : 32 * q + 4, :].bitcast(I32),
             )

@@ -24,7 +24,7 @@ DY_CHUNK = 256
 EARLY_PLANES = (2, 0)
 LATE_PLANES = (1, 3)
 EARLY_SLICES = ((0, 256), (256, 512), (512, 1024))
-OUT_CHUNKS = ((0, 512), (512, 896), (896, 1408), (1408, 1792), (1792, 2048))
+OUT_CHUNKS = ((0, 512), (512, 1024), (1024, 1536), (1536, 1792), (1792, 2048))
 VECTOR_CHUNKS = 2
 ACC_BANK = (0, 1, 2, 3, 0, 1, 2, 3)
 LATE_BANK = (2, 3, 6, 7)

from contextlib import ExitStack

import concourse.mybir as mybir
from concourse.masks import make_identity

K, N, T, J = 512, 512, 2048, 1024
FLOPS = 2 * 2 * K * N * J

F32 = mybir.dt.float32
BF16 = mybir.dt.bfloat16
I32 = mybir.dt.int32
U32 = mybir.dt.uint32
U16 = mybir.dt.uint16
U8 = mybir.dt.uint8
E5M2X4 = mybir.dt.float8_e5m2_x4
E4M3X4 = mybir.dt.float8_e4m3fn_x4
E2M1X4 = mybir.dt.float4_e2m1fn_x4
COPY = mybir.ActivationFunctionType.Copy
MULT = mybir.AluOpType.mult

P = 128
PACK = 4
DY_CHUNK = 256
EARLY_PLANES = (2, 0)
LATE_PLANES = (1, 3)
EARLY_SLICES = ((0, 256), (256, 512), (512, 1024))
OUT_CHUNKS = ((0, 512), (512, 1024), (1024, 1536), (1536, 1792), (1792, 2048))
VECTOR_CHUNKS = 2
ACC_BANK = (0, 1, 2, 3, 0, 1, 2, 3)
LATE_BANK = (2, 3, 6, 7)


def tile_list_embg_res_mulP_kernel(
    tc, dy, w4_words, w4_scales, w8_words, w8_scales, d, wgo, offs, out_0, out_1, out_2
):
    nc = tc.nc
    with ExitStack() as ctx:
        keep = ctx.enter_context(tc.tile_pool(name="keep", bufs=1))
        psum = ctx.enter_context(tc.psum_pool(name="psum", bufs=1))

        offsets = keep.tile([P, J // 16], U16, name="offsets")
        w_scales = keep.tile([P, 2 * N], U8, name="w_scales", align_bytes=64)
        wgo_rows = keep.tile([P, 32], F32, name="wgo_rows", align_bytes=64)
        w4 = keep.tile([P, 2 * N], U8, name="w4", align_bytes=64)
        w8 = keep.tile([P, N], U32, name="w8", align_bytes=64)
        identity = keep.tile([P, P], F32, name="identity")
        page_a = keep.tile([P, T], F32, name="page_a")
        page_b = keep.tile([P, T], F32, name="page_b")
        page_c = keep.tile([P, T], F32, name="page_c")

        for page in (page_a, page_b, page_c):
            nc.vector.memset(page[:].bitcast(I32), 0)
        make_identity(nc, identity[:])

        dy_rows = dy.rearrange("(p i) j -> p i j", i=PACK)
        d_rows = d.rearrange("(p i) j -> p i j", i=PACK)
        out_rows = out_0.rearrange("(p i) t -> p i t", i=PACK)

        n_chunks = J // DY_CHUNK
        dy_raw = [keep.tile([P, PACK, DY_CHUNK], F32, name="dy_raw%d" % b) for b in range(n_chunks)]

        def load_dy(b):
            nc.sync.dma_start(out=dy_raw[b][:], in_=dy_rows[:, :, b * DY_CHUNK : (b + 1) * DY_CHUNK])

        def load_scales(half, src):
            for q in range(4):
                nc.sync.dma_start(
                    out=w_scales[32 * q : 32 * (q + 1), half * N : (half + 1) * N].bitcast(I32),
                    in_=src[0, 4 * q : 4 * q + 4, :].bitcast(I32).partition_broadcast(8),
                )

        nc.sync.dma_start(out=wgo_rows[:], in_=wgo.rearrange("r (c a x) -> a (r c) x", a=4, x=32)[:, 0:32, :])
        load_scales(0, w4_scales)
        load_dy(0)
        nc.sync.dma_start(out=w4[:].bitcast(I32), in_=w4_words[0].bitcast(I32))
        nc.sync.dma_start(out=w8[:].bitcast(I32), in_=w8_words[0].rearrange("p n i -> p (n i)").bitcast(I32))
        load_scales(1, w8_scales)
        load_dy(1)
        load_dy(2)
        load_dy(3)
        d_head = keep.tile([P, 2, DY_CHUNK], F32, name="d_head")
        nc.sync.dma_start(out=d_head[:], in_=d_rows[:, 0:PACK:2, 0:DY_CHUNK])
        nc.sync.dma_start(offsets[:], offs)
        d_rest = keep.tile([P, 2, J - DY_CHUNK], F32, name="d_rest")
        nc.sync.dma_start(out=d_rest[:], in_=d_rows[:, 0:PACK:2, DY_CHUNK:J])

        wgo_col = keep.tile([P, 32], F32, name="wgo_col", align_bytes=64)
        nc.vector.transpose(wgo_col[:], wgo_rows[:])

        dy_codes, dy_scales = [], []
        blocks = DY_CHUNK // P
        for b in range(n_chunks):
            rounded = []
            for h in range(blocks):
                c = b * blocks + h
                tile_c = keep.tile([P, P * PACK], BF16, name="dy_grouped%d" % c, align_bytes=64)
                nc.vector.tensor_copy(
                    out=tile_c[:].rearrange("p (c e i) -> p c i e", e=2, i=PACK),
                    in_=dy_raw[b][:, :, h * P : (h + 1) * P].rearrange("p i (c e) -> p c i e", e=2),
                )
                rounded.append(tile_c)
            for h in range(blocks):
                c = b * blocks + h
                codes = keep.tile([P, P], U32, name="dy_codes%d" % c, align_bytes=64)
                scales = keep.tile([P, P], U8, name="dy_scales%d" % c, align_bytes=64)
                nc.vector.quantize_mx(out=codes[:].bitcast(E5M2X4), scales=scales[:], in_=rounded[h][:])
                dy_codes.append(codes)
                dy_scales.append(scales)

        dxw_t = []

        def multiply(c):
            acc = psum.tile([P, N], F32, name="acc", tag="bank%d" % ACC_BANK[c])
            lhs = dy_codes[c][:].bitcast(E5M2X4)
            lhs_scale = dy_scales[c][:]
            nc.tensor.matmul_mx(
                out=acc[:], lhsT=lhs, lhsT_scale=lhs_scale,
                rhs=w4[:].bitcast(E2M1X4), rhs_scale=w_scales[:, 0:N], start=True, stop=False,
            )
            nc.tensor.matmul_mx(
                out=acc[:], lhsT=lhs, lhsT_scale=lhs_scale,
                rhs=w8[:].bitcast(E4M3X4), rhs_scale=w_scales[:, N : 2 * N], start=False, stop=True,
            )
            staged = keep.tile([P, PACK, P], F32, name="dxw_t%d" % c, tag="dxw_t%d" % c, align_bytes=64)
            nc.scalar.activation(
                out=staged[:], in_=acc[:].rearrange("j (p i) -> j i p", i=PACK),
                func=COPY, scale=wgo_col[:, c : c + 1],
            )
            dxw_t.append(staged)

        def turn(i, lo, hi, dst, bank_no):
            bank = psum.tile([P, hi - lo], F32, name="turned", tag="bank%d" % bank_no)
            for c in range(lo // P, hi // P):
                nc.tensor.transpose(bank[:, c * P - lo : (c + 1) * P - lo], dxw_t[c][:, i, :], identity[:])
            nc.scalar.copy(out=dst, in_=bank[:])

        early_parts = {}
        for s, (lo, hi) in enumerate(EARLY_SLICES):
            for c in range(lo // P, hi // P):
                multiply(c)
            for a, i in enumerate(EARLY_PLANES):
                early_parts[i, lo] = keep.tile([P, hi - lo], F32, name="dxw%d_%d" % (i, lo))
                turn(i, lo, hi, early_parts[i, lo][:], 2 + 2 * s + a)
        dxw_late = {}
        for a, i in enumerate(LATE_PLANES):
            dxw_late[i] = keep.tile([P, J], F32, name="dxw%d" % i)
            for h in range(2):
                turn(i, h * N, (h + 1) * N, dxw_late[i][:, h * N : (h + 1) * N], LATE_BANK[2 * a + h])

        d_late = {}
        for a, i in enumerate(LATE_PLANES):
            d_late[i] = keep.tile([P, J], F32, name="d_late%d" % i, tag="dxw_t%d" % (J // P - 2 - a), align_bytes=64)
            nc.scalar.dma_start(out=d_late[i][:], in_=d_rows[:, i, :])

        grouped_all = keep.tile([P, T * PACK], BF16, name="out_grouped", tag="dxw_t%d" % (J // P - 1), align_bytes=64)

        def grouped(lo, hi):
            return grouped_all[:, lo * PACK : hi * PACK].rearrange("p (t i) -> p t i", i=PACK)

        split = OUT_CHUNKS[VECTOR_CHUNKS][0]
        staged_chunks = range(VECTOR_CHUNKS, len(OUT_CHUNKS))
        pair = {}
        for m in staged_chunks:
            pair[m] = keep.tile([P, 2, OUT_CHUNKS[m][1] - OUT_CHUNKS[m][0]], F32, name="pair%d" % m)
        pages = dict(zip(EARLY_PLANES + LATE_PLANES, (page_a, page_b, page_c, page_a)))

        def round_columns(copy, i, lo, hi):
            copy(out=grouped(lo, hi)[:, :, i], in_=pages[i][:, lo:hi])

        for lo, hi in EARLY_SLICES:
            for i in EARLY_PLANES:
                d_part = d_head[:, i // 2, :] if lo == 0 else d_rest[:, i // 2, lo - DY_CHUNK : hi - DY_CHUNK]
                nc.vector.tensor_tensor(
                    pages[i][:].indirect(offsets[:, lo // 16 : hi // 16]), early_parts[i, lo][:], d_part, MULT
                )
        for i in EARLY_PLANES:
            for m in staged_chunks:
                lo, hi = OUT_CHUNKS[m]
                nc.sync.dma_start(out=pair[m][:, i // 2, :], in_=pages[i][:, lo:hi])
        for i in EARLY_PLANES:
            nc.sync.dma_start(out=out_rows[:, i, :], in_=pages[i][:])
            round_columns(nc.scalar.copy, i, 0, split)
        for m in staged_chunks:
            nc.scalar.copy(
                out=grouped(*OUT_CHUNKS[m])[:, :, 0:PACK:2].rearrange("p (c e) a -> p c a e", e=2),
                in_=pair[m][:].rearrange("p a (c e) -> p c a e", e=2),
            )

        for i in LATE_PLANES:
            nc.vector.tensor_tensor(pages[i][:].indirect(offsets[:]), dxw_late[i][:], d_late[i][:], MULT)
            nc.sync.dma_start(out=out_rows[:, i, :], in_=pages[i][:])
            if i == LATE_PLANES[0]:
                round_columns(nc.scalar.copy, i, 0, T)
            else:
                for m, (lo, hi) in enumerate(OUT_CHUNKS):
                    round_columns(nc.vector.tensor_copy if m < VECTOR_CHUNKS else nc.scalar.copy, i, lo, hi)

        out_scales = keep.tile([P, T], U8, name="out_scales", align_bytes=64)
        words_hbm = out_1[0].rearrange("p t i -> p (t i)").bitcast(I32)
        for m, (lo, hi) in enumerate(OUT_CHUNKS):
            codes = keep.tile([P, hi - lo], U32, name="out_codes%d" % lo, align_bytes=64)
            nc.vector.quantize_mx(
                out=codes[:].bitcast(E4M3X4), scales=out_scales[:, lo:hi],
                in_=grouped_all[:, lo * PACK : hi * PACK],
            )
            nc.sync.dma_start(out=words_hbm[:, lo:hi], in_=codes[:].bitcast(I32))
        for q in range(4):
            nc.sync.dma_start(
                out=out_2[0, 4 * q : 4 * q + 4, :].bitcast(I32),
                in_=out_scales[32 * q : 32 * q + 4, :].bitcast(I32),
            )
